import numpy as np
import ml_dtypes


def mxq(x, axis, fmt="e4m3"):
    dtype, down = {"e4m3": (ml_dtypes.float8_e4m3fn, 7), "e5m2": (ml_dtypes.float8_e5m2, 14)}[fmt]
    v = np.moveaxis(np.asarray(x, np.float32).astype(ml_dtypes.bfloat16).astype(np.float64), axis, -1)
    blocks = v.reshape(v.shape[:-1] + (-1, 32))
    amax = np.abs(blocks).max(-1, keepdims=True)
    byte = np.maximum(np.where(amax > 0, np.frexp(amax)[1] - 1 + 127, 0) - down, 1)
    scale = np.exp2(byte - 127.0)
    codes = (blocks / scale).astype(np.float32).astype(dtype).astype(np.float64)
    return np.moveaxis((codes * scale).reshape(v.shape), -1, axis)


WIDE = False


def mx_kscale(k):
    if not WIDE:
        return np.ones(k)
    levels = np.array([10, -10, 5, -5, 0])
    if k % 512:
        return np.exp2(np.random.permutation(np.resize(levels, k // 32))).repeat(32)
    a = np.empty((k // 512, 16))
    for p in range(k // 512):
        a[p, :8] = np.random.permutation(np.resize(levels, 8))
        for g in range(8):
            far = levels[np.abs(levels - a[p, g]) >= 10]
            a[p, g + 8] = far[np.random.randint(len(far))]
    return np.exp2(a.ravel()).repeat(32)


def f64(x):
    return np.asarray(x).astype(np.float64)


def striped(idx):
    return np.tile(idx.reshape(-1, 16).T, (8, 1)).astype(np.uint16)


def unstriped(offs):
    return offs[:16].T.reshape(-1).astype(np.int64)


K, T, E, C, N = 1024, 1024, 2, 256, 512


def by_expert(wq, xq):
    return np.concatenate([wq[e].T @ xq[:, e * C:(e + 1) * C] for e in range(E)], axis=1)


def setup_inputs():
    n = np.random.standard_normal
    s = mx_kscale(K)[:, None]
    return {
        "xT": (n((K, T)) * s).astype(np.float32),
        "w": (n((E, K, N)) / np.sqrt(K) / s[None]).astype(np.float32),
        "gate": np.tile(np.random.uniform(0.2, 1.0, E * C), (N, 1)).astype(np.float32),
        "offs": striped(np.random.permutation(T)[:E * C]),
    }


def reference(xT, w, gate, offs):
    idx = unstriped(offs)
    xq = mxq(f64(xT)[:, idx], 0, "e4m3")
    y = by_expert(mxq(f64(w), 1, "e4m3"), xq)
    out = np.zeros((N, T))
    out[:, idx] = f64(gate) * y
    return out

@@ -1,0 +1,179 @@
+from contextlib import ExitStack
+
+import concourse.mybir as mybir
+
+K, T, E, C, N = 1024, 1024, 2, 256, 512
+FLOPS = 2 * K * N * E * C
+
+F32 = mybir.dt.float32
+BF16 = mybir.dt.bfloat16
+U32 = mybir.dt.uint32
+U16 = mybir.dt.uint16
+U8 = mybir.dt.uint8
+FP8X4 = mybir.dt.float8_e4m3fn_x4
+MULT = mybir.AluOpType.mult
+ADD = mybir.AluOpType.add
+COPY = mybir.ActivationFunctionType.Copy
+LAST_PIECES = 2
+SPLIT_LAST = 2
+LAG = 2
+
+P = 128
+PACK = 4
+K_PASS = P * PACK
+PASSES = K // K_PASS
+BLOCKS = N // P
+SLOTS = E * C
+XS = 608
+HELPER = "gpsimd"
+JOBS = [(0, (0,)), (0, (1,)), (1, (0,)), (1, (1,)), (2, (0, 1)), (3, (0,)), (3, (1,))]
+FINE = 0
+GATE_AFTER = 1
+AHEAD = 0
+
+
+def tile_routed_moe_kernel(tc, xT, w, gate, offs, out):
+    nc = tc.nc
+    with ExitStack() as ctx:
+        keep = ctx.enter_context(tc.tile_pool(name="keep", bufs=1))
+        psum = ctx.enter_context(tc.psum_pool(name="psum", bufs=1))
+        placed = ctx.enter_context(tc.tile_pool(name="placed", bufs=1))
+
+        offsets = keep.tile([P, SLOTS // 16], U16, name="offsets")
+        nc.sync.dma_start(offsets[:], offs)
+
+        def pieces(g, u):
+            if g == PASSES - 1 and u == 1:
+                return [(k * T // LAST_PIECES, (k + 1) * T // LAST_PIECES) for k in range(LAST_PIECES)]
+            return [(0, T)]
+
+        x_view = xT.rearrange("(g p u e) n -> g u p e n", g=PASSES, p=P, u=2, e=2)
+        x_raw = {}
+        for g in range(PASSES):
+            for u in range(2):
+                x_raw[g, u] = keep.tile([P, 2, T], F32, name="x_raw%d%d" % (g, u))
+                for lo, hi in pieces(g, u):
+                    nc.sync.dma_start(out=x_raw[g, u][:, :, lo:hi], in_=x_view[g, u, :, :, lo:hi])
+        w_view = w.rearrange("e (g p j) c -> e g p j c", g=PASSES, p=P, j=PACK)
+        w_raw = []
+        gate_sb = keep.tile([P, SLOTS], F32, name="gate_sb")
+        for i, (nb, es) in enumerate(JOBS):
+            w_raw.append(keep.tile([P, len(es) * PASSES, PACK, P], F32, name="w_raw%d" % i))
+            for k, e in enumerate(es):
+                for g in range(PASSES):
+                    nc.sync.dma_start(out=w_raw[i][:, k * PASSES + g], in_=w_view[e, g, :, :, nb * P:(nb + 1) * P])
+            if i == GATE_AFTER:
+                nc.sync.dma_start(out=gate_sb[:], in_=gate[0:P, :])
+
+        win = []
+        for nb in range(BLOCKS):
+            win.append(keep.tile([P, T], F32, name="win%d" % nb))
+            nc.vector.memset(win[nb][:], 0.0)
+
+        x_codes = []
+        x_scales = []
+        for g in range(PASSES):
+            xg = keep.tile([P, SLOTS, PACK], BF16, name="xg%d" % g, align_bytes=64)
+            xg_words = xg[:].rearrange("p c t -> p (c t)").bitcast(U32).rearrange("p (c u) -> p c u", u=2)
+            for u in range(2):
+                pairs = keep.tile([P, T, 2], BF16, name="pairs%d%d" % (g, u), align_bytes=64)
+                for lo, hi in pieces(g, u):
+                    cut = lo + (hi - lo) * XS // T
+                    nc.scalar.copy(out=pairs[:, lo:cut, :], in_=x_raw[g, u][:, :, lo:cut].rearrange("p e n -> p n e"))
+                    nc.gpsimd.tensor_scalar(
+                        out=pairs[:, cut:hi, :],
+                        in0=x_raw[g, u][:, :, cut:hi].rearrange("p e n -> p n e"),
+                        scalar1=1.0, scalar2=0.0, op0=MULT, op1=ADD,
+                    )
+                window = pairs[:].rearrange("p n e -> p (n e)").bitcast(U32)
+                halves = SPLIT_LAST if (g == PASSES - 1 and u == 1) else 1
+                for h in range(halves):
+                    c0, c1 = h * SLOTS // halves, (h + 1) * SLOTS // halves
+                    nc.vector.tensor_copy(out=xg_words[:, c0:c1, u], in_=window.indirect(offsets[:, c0 // 16:c1 // 16]))
+            x_codes.append(keep.tile([P, SLOTS], U32, name="x_codes%d" % g, align_bytes=64))
+            x_scales.append(keep.tile([P, SLOTS], U8, name="x_scales%d" % g, align_bytes=64))
+            halves = SPLIT_LAST if g == PASSES - 1 else 1
+            for h in range(halves):
+                c0, c1 = h * SLOTS // halves, (h + 1) * SLOTS // halves
+                nc.vector.quantize_mx(
+                    out=x_codes[g][:, c0:c1].bitcast(FP8X4),
+                    scales=x_scales[g][:, c0:c1],
+                    in_=xg[:, c0:c1, :].rearrange("p c t -> p (c t)"),
+                )
+
+        acc = {}
+
+        wb = {}
+
+        def wb_offset(i):
+            return sum(len(es) * PASSES * P * PACK * 2 for nb, es in JOBS[:i])
+
+        def cast(i):
+            nb, es = JOBS[i]
+            parts = len(es) * PASSES
+            wb[i] = placed.tile([P, parts, P, PACK], BF16, name="wb%d" % i, offset=wb_offset(i))
+            step = 1 if i < FINE else PASSES
+            for a in range(0, parts, step):
+                nc.scalar.copy(
+                    out=wb[i][:, a:a + step].rearrange("p a (c i) j -> p a c j i", i=4),
+                    in_=w_raw[i][:, a:a + step].rearrange("p a j (c i) -> p a c j i", i=4),
+                )
+
+        def multiply(i):
+            nb, es = JOBS[i]
+            parts = len(es) * PASSES
+            w_codes = keep.tile([P, parts * P], U32, name="w_codes%d" % i, align_bytes=64)
+            w_scales = keep.tile([P, parts * P], U8, name="w_scales%d" % i, align_bytes=64)
+            nc.vector.quantize_mx(
+                out=w_codes[:].bitcast(FP8X4),
+                scales=w_scales[:],
+                in_=wb[i][:].rearrange("p a m j -> p (a m j)"),
+            )
+            acc[i] = psum.tile([P, len(es) * C], F32, name="acc%d" % i)
+            for k, e in enumerate(es):
+                for g in range(PASSES):
+                    a = k * PASSES + g
+                    nc.tensor.matmul_mx(
+                        out=acc[i][:, k * C:(k + 1) * C],
+                        lhsT=w_codes[:, a * P:(a + 1) * P].bitcast(FP8X4),
+                        lhsT_scale=w_scales[:, a * P:(a + 1) * P],
+                        rhs=x_codes[g][:, e * C:(e + 1) * C].bitcast(FP8X4),
+                        rhs_scale=x_scales[g][:, e * C:(e + 1) * C],
+                        start=(g == 0),
+                        stop=(g == PASSES - 1),
+                    )
+
+        y = {}
+
+        def empty(i):
+            nb, es = JOBS[i]
+            y[i] = keep.tile([P, len(es) * C], F32, name="y%d" % i)
+            if i + LAG < len(JOBS):
+                mark = placed.tile([P, 1], F32, name="mark%d" % i, offset=wb_offset(i + LAG))
+                nc.scalar.activation(out=y[i][:], in_=acc[i][:], func=COPY, accum_out=mark[:])
+            else:
+                nc.scalar.copy(out=y[i][:], in_=acc[i][:])
+
+        def scatter(i):
+            nb, es = JOBS[i]
+            lo, hi = es[0], es[-1] + 1
+            nc.vector.tensor_tensor(
+                out=win[nb][:].indirect(offsets[:, lo * (C // 16):hi * (C // 16)]),
+                in0=y[i][:],
+                in1=gate_sb[:, lo * C:hi * C],
+                op=MULT,
+            )
+            if hi == E:
+                nc.sync.dma_start(out=out[nb * P:(nb + 1) * P, :], in_=win[nb][:])
+
+        n = len(JOBS)
+        cast(0)
+        cast(1)
+        multiply(0)
+        for i in range(n):
+            empty(i)
+            if i + 2 < n:
+                cast(i + 2)
+            if i + 1 < n:
+                multiply(i + 1)
+            scatter(i)

@@ -71,35 +71,46 @@ def tile_routed_moe_kernel(tc, xT, w, gate, offs, out):
             nc.vector.memset(win[nb][:], 0.0)
 
         x_codes = []
-        x_scales = []
+        x_scales = {}
+        xg = []
+        window = {}
         for g in range(PASSES):
-            xg = keep.tile([P, SLOTS, PACK], BF16, name="xg%d" % g, align_bytes=64)
-            xg_words = xg[:].rearrange("p c t -> p (c t)").bitcast(U32).rearrange("p (c u) -> p c u", u=2)
-            for u in range(2):
-                pairs = keep.tile([P, T, 2], BF16, name="pairs%d%d" % (g, u), align_bytes=64)
-                for lo, hi in pieces(g, u):
-                    cut = lo + (hi - lo) * XS // T
-                    nc.scalar.copy(out=pairs[:, lo:cut, :], in_=x_raw[g, u][:, :, lo:cut].rearrange("p e n -> p n e"))
-                    nc.gpsimd.tensor_scalar(
-                        out=pairs[:, cut:hi, :],
-                        in0=x_raw[g, u][:, :, cut:hi].rearrange("p e n -> p n e"),
-                        scalar1=1.0, scalar2=0.0, op0=MULT, op1=ADD,
-                    )
-                window = pairs[:].rearrange("p n e -> p (n e)").bitcast(U32)
-                halves = SPLIT_LAST if (g == PASSES - 1 and u == 1) else 1
-                for h in range(halves):
-                    c0, c1 = h * SLOTS // halves, (h + 1) * SLOTS // halves
-                    nc.vector.tensor_copy(out=xg_words[:, c0:c1, u], in_=window.indirect(offsets[:, c0 // 16:c1 // 16]))
+            xg.append(keep.tile([P, SLOTS, PACK], BF16, name="xg%d" % g, align_bytes=64))
             x_codes.append(keep.tile([P, SLOTS], U32, name="x_codes%d" % g, align_bytes=64))
-            x_scales.append(keep.tile([P, SLOTS], U8, name="x_scales%d" % g, align_bytes=64))
-            halves = SPLIT_LAST if g == PASSES - 1 else 1
-            for h in range(halves):
-                c0, c1 = h * SLOTS // halves, (h + 1) * SLOTS // halves
-                nc.vector.quantize_mx(
-                    out=x_codes[g][:, c0:c1].bitcast(FP8X4),
-                    scales=x_scales[g][:, c0:c1],
-                    in_=xg[:, c0:c1, :].rearrange("p c t -> p (c t)"),
+
+        def round_tokens(g, u):
+            pairs = keep.tile([P, T, 2], BF16, name="pairs%d%d" % (g, u), align_bytes=64)
+            for lo, hi in pieces(g, u):
+                cut = lo + (hi - lo) * XS // T
+                nc.scalar.copy(out=pairs[:, lo:cut, :], in_=x_raw[g, u][:, :, lo:cut].rearrange("p e n -> p n e"))
+                nc.gpsimd.tensor_scalar(
+                    out=pairs[:, cut:hi, :],
+                    in0=x_raw[g, u][:, :, cut:hi].rearrange("p e n -> p n e"),
+                    scalar1=1.0, scalar2=0.0, op0=MULT, op1=ADD,
                 )
+            window[g, u] = pairs[:].rearrange("p n e -> p (n e)").bitcast(U32)
+
+        def gather(g, u, c0, c1):
+            xg_words = xg[g][:].rearrange("p c t -> p (c t)").bitcast(U32).rearrange("p (c u) -> p c u", u=2)
+            nc.vector.tensor_copy(out=xg_words[:, c0:c1, u], in_=window[g, u].indirect(offsets[:, c0 // 16:c1 // 16]))
+
+        def quantize_tokens(g, e):
+            if e == 0:
+                x_scales[g, e] = keep.tile([P, C], U8, name="x_scales%d%d" % (g, e), align_bytes=64)
+            else:
+                x_scales[g, e] = placed.tile([P, C], U8, name="x_scales%d%d" % (g, e), offset=g * C)
+            nc.vector.quantize_mx(
+                out=x_codes[g][:, e * C:(e + 1) * C].bitcast(FP8X4),
+                scales=x_scales[g, e][:],
+                in_=xg[g][:, e * C:(e + 1) * C, :].rearrange("p c t -> p (c t)"),
+            )
+
+        for g, u in ((0, 0), (0, 1), (1, 0)):
+            round_tokens(g, u)
+            gather(g, u, 0, SLOTS)
+            if (g, u) == (0, 1):
+                quantize_tokens(0, 0)
+        round_tokens(1, 1)
 
         acc = {}
 
@@ -119,26 +130,32 @@ def tile_routed_moe_kernel(tc, xT, w, gate, offs, out):
                     in_=w_raw[i][:, a:a + step].rearrange("p a j (c i) -> p a c j i", i=4),
                 )
 
-        def multiply(i):
+        w_codes = {}
+        w_scales = {}
+
+        def quantize_weights(i):
             nb, es = JOBS[i]
             parts = len(es) * PASSES
-            w_codes = keep.tile([P, parts * P], U32, name="w_codes%d" % i, align_bytes=64)
-            w_scales = keep.tile([P, parts * P], U8, name="w_scales%d" % i, align_bytes=64)
+            w_codes[i] = keep.tile([P, parts * P], U32, name="w_codes%d" % i, align_bytes=64)
+            w_scales[i] = keep.tile([P, parts * P], U8, name="w_scales%d" % i, align_bytes=64)
             nc.vector.quantize_mx(
-                out=w_codes[:].bitcast(FP8X4),
-                scales=w_scales[:],
+                out=w_codes[i][:].bitcast(FP8X4),
+                scales=w_scales[i][:],
                 in_=wb[i][:].rearrange("p a m j -> p (a m j)"),
             )
+
+        def matmuls(i):
+            nb, es = JOBS[i]
             acc[i] = psum.tile([P, len(es) * C], F32, name="acc%d" % i)
             for k, e in enumerate(es):
                 for g in range(PASSES):
                     a = k * PASSES + g
                     nc.tensor.matmul_mx(
                         out=acc[i][:, k * C:(k + 1) * C],
-                        lhsT=w_codes[:, a * P:(a + 1) * P].bitcast(FP8X4),
-                        lhsT_scale=w_scales[:, a * P:(a + 1) * P],
+                        lhsT=w_codes[i][:, a * P:(a + 1) * P].bitcast(FP8X4),
+                        lhsT_scale=w_scales[i][:, a * P:(a + 1) * P],
                         rhs=x_codes[g][:, e * C:(e + 1) * C].bitcast(FP8X4),
-                        rhs_scale=x_scales[g][:, e * C:(e + 1) * C],
+                        rhs_scale=x_scales[g, e][:],
                         start=(g == 0),
                         stop=(g == PASSES - 1),
                     )
@@ -169,11 +186,18 @@ def tile_routed_moe_kernel(tc, xT, w, gate, offs, out):
         n = len(JOBS)
         cast(0)
         cast(1)
-        multiply(0)
+        gather(1, 1, 0, C)
+        gather(1, 1, C, SLOTS)
+        quantize_tokens(1, 0)
+        quantize_weights(0)
+        matmuls(0)
+        quantize_tokens(0, 1)
+        quantize_tokens(1, 1)
         for i in range(n):
             empty(i)
             if i + 2 < n:
                 cast(i + 2)
             if i + 1 < n:
-                multiply(i + 1)
+                quantize_weights(i + 1)
+                matmuls(i + 1)
             scatter(i)

@@ -26,7 +26,7 @@ BLOCKS = N // P
 SLOTS = E * C
 XS = 608
 HELPER = "gpsimd"
-JOBS = [(0, (0,)), (0, (1,)), (1, (0,)), (1, (1,)), (2, (0, 1)), (3, (0,)), (3, (1,))]
+JOBS = [(0, (0,)), (0, (1,)), (1, (0,)), (1, (1,)), (2, (0,)), (2, (1,)), (3, (0,)), (3, (1,))]
 FINE = 0
 GATE_AFTER = 1
 AHEAD = 0

@@ -98,7 +98,7 @@ def tile_routed_moe_kernel(tc, xT, w, gate, offs, out):
             if e == 0:
                 x_scales[g, e] = keep.tile([P, C], U8, name="x_scales%d%d" % (g, e), align_bytes=64)
             else:
-                x_scales[g, e] = placed.tile([P, C], U8, name="x_scales%d%d" % (g, e), offset=g * C)
+                x_scales[g, e] = placed.tile([P, C], U8, name="x_scales%d%d" % (g, e), offset=g * C, align_bytes=64)
             nc.vector.quantize_mx(
                 out=x_codes[g][:, e * C:(e + 1) * C].bitcast(FP8X4),
                 scales=x_scales[g, e][:],
@@ -122,7 +122,7 @@ def tile_routed_moe_kernel(tc, xT, w, gate, offs, out):
         def cast(i):
             nb, es = JOBS[i]
             parts = len(es) * PASSES
-            wb[i] = placed.tile([P, parts, P, PACK], BF16, name="wb%d" % i, offset=wb_offset(i))
+            wb[i] = placed.tile([P, parts, P, PACK], BF16, name="wb%d" % i, offset=wb_offset(i), align_bytes=64)
             step = 1 if i < FINE else PASSES
             for a in range(0, parts, step):
                 nc.scalar.copy(

@@ -26,7 +26,7 @@ BLOCKS = N // P
 SLOTS = E * C
 XS = 608
 HELPER = "gpsimd"
-JOBS = [(0, (0,)), (0, (1,)), (1, (0,)), (1, (1,)), (2, (0,)), (2, (1,)), (3, (0,)), (3, (1,))]
+JOBS = [(0, (0,)), (1, (0,)), (2, (0,)), (3, (0,)), (0, (1,)), (1, (1,)), (2, (1,)), (3, (1,))]
 FINE = 0
 GATE_AFTER = 1
 AHEAD = 0

@@ -24,7 +24,7 @@ K_PASS = P * PACK
 PASSES = K // K_PASS
 BLOCKS = N // P
 SLOTS = E * C
-XS = 608
+XS = 512
 HELPER = "gpsimd"
 JOBS = [(0, (0,)), (1, (0,)), (2, (0,)), (3, (0,)), (0, (1,)), (1, (1,)), (2, (1,)), (3, (1,))]
 FINE = 0

@@ -40,7 +40,6 @@ def tile_routed_moe_kernel(tc, xT, w, gate, offs, out):
         placed = ctx.enter_context(tc.tile_pool(name="placed", bufs=1))
 
         offsets = keep.tile([P, SLOTS // 16], U16, name="offsets")
-        nc.sync.dma_start(offsets[:], offs)
 
         def pieces(g, u):
             if g == PASSES - 1 and u == 1:
@@ -54,6 +53,8 @@ def tile_routed_moe_kernel(tc, xT, w, gate, offs, out):
                 x_raw[g, u] = keep.tile([P, 2, T], F32, name="x_raw%d%d" % (g, u))
                 for lo, hi in pieces(g, u):
                     nc.sync.dma_start(out=x_raw[g, u][:, :, lo:hi], in_=x_view[g, u, :, :, lo:hi])
+                if (g, u) == (0, 0):
+                    nc.sync.dma_start(offsets[:], offs)
         w_view = w.rearrange("e (g p j) c -> e g p j c", g=PASSES, p=P, j=PACK)
         w_raw = []
         gate_sb = keep.tile([P, SLOTS], F32, name="gate_sb")

@@ -30,6 +30,7 @@ JOBS = [(0, (0,)), (1, (0,)), (2, (0,)), (3, (0,)), (0, (1,)), (1, (1,)), (2, (1
 FINE = 0
 GATE_AFTER = 1
 AHEAD = 0
+RUN = 8
 
 
 def tile_routed_moe_kernel(tc, xT, w, gate, offs, out):
@@ -127,8 +128,8 @@ def tile_routed_moe_kernel(tc, xT, w, gate, offs, out):
             step = 1 if i < FINE else PASSES
             for a in range(0, parts, step):
                 nc.scalar.copy(
-                    out=wb[i][:, a:a + step].rearrange("p a (c i) j -> p a c j i", i=4),
-                    in_=w_raw[i][:, a:a + step].rearrange("p a j (c i) -> p a c j i", i=4),
+                    out=wb[i][:, a:a + step].rearrange("p a (c i) j -> p a c j i", i=RUN),
+                    in_=w_raw[i][:, a:a + step].rearrange("p a j (c i) -> p a c j i", i=RUN),
                 )
 
         w_codes = {}

@@ -14,7 +14,7 @@ FP8X4 = mybir.dt.float8_e4m3fn_x4
 MULT = mybir.AluOpType.mult
 ADD = mybir.AluOpType.add
 COPY = mybir.ActivationFunctionType.Copy
-LAST_PIECES = 2
+LAST_CUTS = (0, 512, 768, 1024)
 SPLIT_LAST = 2
 LAG = 2
 
@@ -44,7 +44,7 @@ def tile_routed_moe_kernel(tc, xT, w, gate, offs, out):
 
         def pieces(g, u):
             if g == PASSES - 1 and u == 1:
-                return [(k * T // LAST_PIECES, (k + 1) * T // LAST_PIECES) for k in range(LAST_PIECES)]
+                return [(LAST_CUTS[k], LAST_CUTS[k + 1]) for k in range(len(LAST_CUTS) - 1)]
             return [(0, T)]
 
         x_view = xT.rearrange("(g p u e) n -> g u p e n", g=PASSES, p=P, u=2, e=2)

from contextlib import ExitStack

import concourse.mybir as mybir

K, T, E, C, N = 1024, 1024, 2, 256, 512
FLOPS = 2 * K * N * E * C

F32 = mybir.dt.float32
BF16 = mybir.dt.bfloat16
U32 = mybir.dt.uint32
U16 = mybir.dt.uint16
U8 = mybir.dt.uint8
FP8X4 = mybir.dt.float8_e4m3fn_x4
MULT = mybir.AluOpType.mult
ADD = mybir.AluOpType.add
COPY = mybir.ActivationFunctionType.Copy
LAST_CUTS = (0, 512, 768, 1024)
SPLIT_LAST = 2
LAG = 2

P = 128
PACK = 4
K_PASS = P * PACK
PASSES = K // K_PASS
BLOCKS = N // P
SLOTS = E * C
XS = 512
HELPER = "gpsimd"
JOBS = [(0, (0,)), (1, (0,)), (2, (0,)), (3, (0,)), (0, (1,)), (1, (1,)), (2, (1,)), (3, (1,))]
FINE = 0
GATE_AFTER = 1
AHEAD = 0
RUN = 8


def tile_routed_moe_kernel(tc, xT, w, gate, offs, out):
    nc = tc.nc
    with ExitStack() as ctx:
        keep = ctx.enter_context(tc.tile_pool(name="keep", bufs=1))
        psum = ctx.enter_context(tc.psum_pool(name="psum", bufs=1))
        placed = ctx.enter_context(tc.tile_pool(name="placed", bufs=1))

        offsets = keep.tile([P, SLOTS // 16], U16, name="offsets")

        def pieces(g, u):
            if g == PASSES - 1 and u == 1:
                return [(LAST_CUTS[k], LAST_CUTS[k + 1]) for k in range(len(LAST_CUTS) - 1)]
            return [(0, T)]

        x_view = xT.rearrange("(g p u e) n -> g u p e n", g=PASSES, p=P, u=2, e=2)
        x_raw = {}
        for g in range(PASSES):
            for u in range(2):
                x_raw[g, u] = keep.tile([P, 2, T], F32, name="x_raw%d%d" % (g, u))
                for lo, hi in pieces(g, u):
                    nc.sync.dma_start(out=x_raw[g, u][:, :, lo:hi], in_=x_view[g, u, :, :, lo:hi])
                if (g, u) == (0, 0):
                    nc.sync.dma_start(offsets[:], offs)
        w_view = w.rearrange("e (g p j) c -> e g p j c", g=PASSES, p=P, j=PACK)
        w_raw = []
        gate_sb = keep.tile([P, SLOTS], F32, name="gate_sb")
        for i, (nb, es) in enumerate(JOBS):
            w_raw.append(keep.tile([P, len(es) * PASSES, PACK, P], F32, name="w_raw%d" % i))
            for k, e in enumerate(es):
                for g in range(PASSES):
                    nc.sync.dma_start(out=w_raw[i][:, k * PASSES + g], in_=w_view[e, g, :, :, nb * P:(nb + 1) * P])
            if i == GATE_AFTER:
                nc.sync.dma_start(out=gate_sb[:], in_=gate[0:P, :])

        win = []
        for nb in range(BLOCKS):
            win.append(keep.tile([P, T], F32, name="win%d" % nb))
            nc.vector.memset(win[nb][:], 0.0)

        x_codes = []
        x_scales = {}
        xg = []
        window = {}
        for g in range(PASSES):
            xg.append(keep.tile([P, SLOTS, PACK], BF16, name="xg%d" % g, align_bytes=64))
            x_codes.append(keep.tile([P, SLOTS], U32, name="x_codes%d" % g, align_bytes=64))

        def round_tokens(g, u):
            pairs = keep.tile([P, T, 2], BF16, name="pairs%d%d" % (g, u), align_bytes=64)
            for lo, hi in pieces(g, u):
                cut = lo + (hi - lo) * XS // T
                nc.scalar.copy(out=pairs[:, lo:cut, :], in_=x_raw[g, u][:, :, lo:cut].rearrange("p e n -> p n e"))
                nc.gpsimd.tensor_scalar(
                    out=pairs[:, cut:hi, :],
                    in0=x_raw[g, u][:, :, cut:hi].rearrange("p e n -> p n e"),
                    scalar1=1.0, scalar2=0.0, op0=MULT, op1=ADD,
                )
            window[g, u] = pairs[:].rearrange("p n e -> p (n e)").bitcast(U32)

        def gather(g, u, c0, c1):
            xg_words = xg[g][:].rearrange("p c t -> p (c t)").bitcast(U32).rearrange("p (c u) -> p c u", u=2)
            nc.vector.tensor_copy(out=xg_words[:, c0:c1, u], in_=window[g, u].indirect(offsets[:, c0 // 16:c1 // 16]))

        def quantize_tokens(g, e):
            if e == 0:
                x_scales[g, e] = keep.tile([P, C], U8, name="x_scales%d%d" % (g, e), align_bytes=64)
            else:
                x_scales[g, e] = placed.tile([P, C], U8, name="x_scales%d%d" % (g, e), offset=g * C, align_bytes=64)
            nc.vector.quantize_mx(
                out=x_codes[g][:, e * C:(e + 1) * C].bitcast(FP8X4),
                scales=x_scales[g, e][:],
                in_=xg[g][:, e * C:(e + 1) * C, :].rearrange("p c t -> p (c t)"),
            )

        for g, u in ((0, 0), (0, 1), (1, 0)):
            round_tokens(g, u)
            gather(g, u, 0, SLOTS)
            if (g, u) == (0, 1):
                quantize_tokens(0, 0)
        round_tokens(1, 1)

        acc = {}

        wb = {}

        def wb_offset(i):
            return sum(len(es) * PASSES * P * PACK * 2 for nb, es in JOBS[:i])

        def cast(i):
            nb, es = JOBS[i]
            parts = len(es) * PASSES
            wb[i] = placed.tile([P, parts, P, PACK], BF16, name="wb%d" % i, offset=wb_offset(i), align_bytes=64)
            step = 1 if i < FINE else PASSES
            for a in range(0, parts, step):
                nc.scalar.copy(
                    out=wb[i][:, a:a + step].rearrange("p a (c i) j -> p a c j i", i=RUN),
                    in_=w_raw[i][:, a:a + step].rearrange("p a j (c i) -> p a c j i", i=RUN),
                )

        w_codes = {}
        w_scales = {}

        def quantize_weights(i):
            nb, es = JOBS[i]
            parts = len(es) * PASSES
            w_codes[i] = keep.tile([P, parts * P], U32, name="w_codes%d" % i, align_bytes=64)
            w_scales[i] = keep.tile([P, parts * P], U8, name="w_scales%d" % i, align_bytes=64)
            nc.vector.quantize_mx(
                out=w_codes[i][:].bitcast(FP8X4),
                scales=w_scales[i][:],
                in_=wb[i][:].rearrange("p a m j -> p (a m j)"),
            )

        def matmuls(i):
            nb, es = JOBS[i]
            acc[i] = psum.tile([P, len(es) * C], F32, name="acc%d" % i)
            for k, e in enumerate(es):
                for g in range(PASSES):
                    a = k * PASSES + g
                    nc.tensor.matmul_mx(
                        out=acc[i][:, k * C:(k + 1) * C],
                        lhsT=w_codes[i][:, a * P:(a + 1) * P].bitcast(FP8X4),
                        lhsT_scale=w_scales[i][:, a * P:(a + 1) * P],
                        rhs=x_codes[g][:, e * C:(e + 1) * C].bitcast(FP8X4),
                        rhs_scale=x_scales[g, e][:],
                        start=(g == 0),
                        stop=(g == PASSES - 1),
                    )

        y = {}

        def empty(i):
            nb, es = JOBS[i]
            y[i] = keep.tile([P, len(es) * C], F32, name="y%d" % i)
            if i + LAG < len(JOBS):
                mark = placed.tile([P, 1], F32, name="mark%d" % i, offset=wb_offset(i + LAG))
                nc.scalar.activation(out=y[i][:], in_=acc[i][:], func=COPY, accum_out=mark[:])
            else:
                nc.scalar.copy(out=y[i][:], in_=acc[i][:])

        def scatter(i):
            nb, es = JOBS[i]
            lo, hi = es[0], es[-1] + 1
            nc.vector.tensor_tensor(
                out=win[nb][:].indirect(offsets[:, lo * (C // 16):hi * (C // 16)]),
                in0=y[i][:],
                in1=gate_sb[:, lo * C:hi * C],
                op=MULT,
            )
            if hi == E:
                nc.sync.dma_start(out=out[nb * P:(nb + 1) * P, :], in_=win[nb][:])

        n = len(JOBS)
        cast(0)
        cast(1)
        gather(1, 1, 0, C)
        gather(1, 1, C, SLOTS)
        quantize_tokens(1, 0)
        quantize_weights(0)
        matmuls(0)
        quantize_tokens(0, 1)
        quantize_tokens(1, 1)
        for i in range(n):
            empty(i)
            if i + 2 < n:
                cast(i + 2)
            if i + 1 < n:
                quantize_weights(i + 1)
                matmuls(i + 1)
            scatter(i)
